import numpy as np
import ml_dtypes


def mxq(x, axis, fmt="e4m3"):
    dtype, down = {"e4m3": (ml_dtypes.float8_e4m3fn, 7), "e5m2": (ml_dtypes.float8_e5m2, 14)}[fmt]
    v = np.moveaxis(np.asarray(x, np.float32).astype(ml_dtypes.bfloat16).astype(np.float64), axis, -1)
    blocks = v.reshape(v.shape[:-1] + (-1, 32))
    amax = np.abs(blocks).max(-1, keepdims=True)
    byte = np.maximum(np.where(amax > 0, np.frexp(amax)[1] - 1 + 127, 0) - down, 1)
    scale = np.exp2(byte - 127.0)
    codes = (blocks / scale).astype(np.float32).astype(dtype).astype(np.float64)
    return np.moveaxis((codes * scale).reshape(v.shape), -1, axis)


WIDE = False


def mx_kscale(k):
    if not WIDE:
        return np.ones(k)
    levels = np.array([30, -30])
    if k % 512:
        return np.exp2(np.random.permutation(np.resize(levels, k // 32))).repeat(32)
    a = np.empty((k // 512, 16))
    for p in range(k // 512):
        a[p, :8] = np.random.permutation(np.resize(levels, 8))
        for g in range(8):
            far = levels[np.abs(levels - a[p, g]) >= 10]
            a[p, g + 8] = far[np.random.randint(len(far))]
    return np.exp2(a.ravel()).repeat(32)


BF16 = ml_dtypes.bfloat16


def bf(x):
    return np.asarray(x, np.float32).astype(BF16)


def f64(x):
    return np.asarray(x).astype(np.float64)


E2M1 = np.array([0.0, 0.5, 1.0, 1.5, 2.0, 3.0, 4.0, 6.0, -0.0, -0.5, -1.0, -1.5, -2.0, -3.0, -4.0, -6.0])


def pack_weight(w, fmt):
    k, n = w.shape
    w = f64(bf(w)).reshape(k // 32, 32, n)
    amax = np.abs(w).max(1)
    if fmt in ("e4m3", "e5m2"):
        byte = np.frexp(amax)[1] - 1 + 127 - (7 if fmt == "e4m3" else 14)
    else:
        mant, ex = np.frexp(amax / 6.0)
        byte = np.where(mant > 0.5, ex, ex - 1) + 127
    byte = np.clip(np.where(amax > 0, byte, 1), 1, 254)
    scaled = (w * np.exp2(127.0 - byte)[:, None, :]).reshape(k, n).astype(np.float32)
    by_word = np.ascontiguousarray(scaled.reshape(k // 512, 128, 4, n).transpose(0, 1, 3, 2))
    if fmt in ("e4m3", "e5m2"):
        words = by_word.astype(ml_dtypes.float8_e4m3fn if fmt == "e4m3" else ml_dtypes.float8_e5m2).view(np.uint8)
    else:
        c = by_word.astype(ml_dtypes.float4_e2m1fn).view(np.uint8) & 0xF
        words = c[..., 0::2] | (c[..., 1::2] << 4)
    return np.ascontiguousarray(words), np.ascontiguousarray(byte.astype(np.uint8).reshape(k // 512, 16, n))


def unpack_weight(words, scales, fmt):
    g, p, n, _ = words.shape
    if fmt in ("e4m3", "e5m2"):
        vals = np.ascontiguousarray(words).view(ml_dtypes.float8_e4m3fn if fmt == "e4m3" else ml_dtypes.float8_e5m2).astype(np.float64)
    else:
        nib = np.empty((g, p, n, 4), np.uint8)
        nib[..., 0::2] = words & 0xF
        nib[..., 1::2] = words >> 4
        vals = E2M1[nib]
    vals = vals * np.repeat(np.exp2(scales.astype(np.float64) - 127.0), 8, axis=1)[..., None]
    return vals.transpose(0, 1, 3, 2).reshape(g * 512, n)

def planes(Y):
    n, m = Y.shape
    b = f64(bf(Y)).reshape(n // 32, 32, m)
    amax = np.abs(b).max(1)
    byte = np.clip(np.where(amax > 0, np.frexp(amax)[1] - 1 + 127 - 7, 1), 1, 254)
    codes = (b * np.exp2(127.0 - byte)[:, None, :]).reshape(n, m).astype(np.float32).astype(ml_dtypes.float8_e4m3fn).view(np.uint8)
    words = codes.reshape(n // 512, 128, 4, m).transpose(0, 1, 3, 2)
    return np.ascontiguousarray(words), np.ascontiguousarray(byte.astype(np.uint8).reshape(n // 512, 16, m))


QUERIES, REFS, FEATS, SCAFFOLDS = 1024, 1536, 2048, 16

def fingerprints(n, scaffold):
    size = np.exp(0.3 * np.random.randn(n, 1))
    pattern = np.tile(scaffold, (n // SCAFFOLDS, 1)) + np.random.randn(n, FEATS)
    return size * np.exp(pattern - 1.0) / np.sqrt(FEATS)

def setup_inputs():
    scaffold = 0.8 * np.random.randn(SCAFFOLDS, FEATS)
    q = fingerprints(QUERIES, scaffold)
    r = fingerprints(REFS, scaffold)
    s = mx_kscale(FEATS)
    q_words, q_scales = pack_weight((q * s).T, "e5m2")
    return {
        "q_words": q_words,
        "q_scales": q_scales,
        "r": bf(r / s),
        "q_self": bf(np.sum(q * q, axis=1)),
        "r_self": bf(np.sum(r * r, axis=1)),
        "gain": bf(3.0 * np.exp(0.8 * np.random.randn(REFS))),
    }

def reference(q_words, q_scales, r, q_self, r_self, gain):
    G = unpack_weight(q_words, q_scales, "e5m2")
    rq = mxq(f64(r), 1, "e4m3")
    inter = G.T @ rq.T
    total = f64(q_self)[:, None] + f64(r_self)[None, :]
    union = total - inter
    sim = inter / union
    y = sim * f64(gain)[None, :]
    Y = y.T
    words, scales = planes(Y)
    return y, words, scales

@@ -1,0 +1,361 @@
+from contextlib import ExitStack
+
+import concourse.mybir as mybir
+from concourse.masks import make_identity
+
+QUERIES, REFS, FEATS = 1024, 1536, 2048
+FLOPS = 2 * QUERIES * REFS * FEATS
+
+F32 = mybir.dt.float32
+BF16 = mybir.dt.bfloat16
+I32 = mybir.dt.int32
+U32 = mybir.dt.uint32
+U8 = mybir.dt.uint8
+E4M3X4 = mybir.dt.float8_e4m3fn_x4
+E5M2X4 = mybir.dt.float8_e5m2_x4
+ALU = mybir.AluOpType
+ACT = mybir.ActivationFunctionType
+
+P = 128
+PACK = 4
+N = 512
+PASSES = FEATS // (P * PACK)
+GROUPS = REFS // (P * PACK)
+HALVES = QUERIES // N
+SLOTS = GROUPS * PACK
+UNITS = GROUPS * HALVES * PACK
+SETS = GROUPS * HALVES
+
+
+def tile_tanimoto_weighted_similarity_planes_k2_kernel(
+    tc, q_words, q_scales, r, q_self, r_self, gain, out_0, out_1, out_2
+):
+    nc = tc.nc
+    with ExitStack() as ctx:
+        keep = ctx.enter_context(tc.tile_pool(name="keep", bufs=1))
+        work = ctx.enter_context(tc.tile_pool(name="work", bufs=3))
+        mx_psum = ctx.enter_context(tc.psum_pool(name="mx_psum", bufs=4))
+        tr_psum = ctx.enter_context(tc.psum_pool(name="tr_psum", bufs=4))
+        ctx.enter_context(tc.manual_schedule())
+
+        ident = keep.tile([P, P], F32, name="ident")
+        g_scales = [keep.tile([P, PASSES, N], U8, name="g_scales%d" % h, align_bytes=64) for h in range(HALVES)]
+        q_cols = keep.tile([P, 8], BF16, name="q_cols")
+        q_cols32 = keep.tile([P, 8], F32, name="q_cols32")
+        q_rows = keep.tile([P, QUERIES], F32, name="q_rows")
+        r_cols = keep.tile([P, GROUPS, PACK], BF16, name="r_cols")
+        gain_cols = keep.tile([P, GROUPS, PACK], BF16, name="gain_cols")
+        warm = keep.tile([P, 1], F32, name="warm")
+        warm_out = keep.tile([P, 1], F32, name="warm_out")
+
+        nc.vector.memset(warm[:], 1.0)
+        for h in range(HALVES):
+            nc.vector.memset(g_scales[h][:].rearrange("p g n -> p (g n)").bitcast(I32), 0)
+        nc.scalar.activation(warm_out[:], warm[:], ACT.Abs_reciprocal_sqrt)
+        make_identity(nc, ident[:])
+
+        raw = {}
+        g_words = {}
+        words_hbm = q_words.rearrange("g p n t -> p g (n t)").bitcast(I32)
+
+        def load_slot(s, pieces):
+            g, t = divmod(s, PACK)
+            rows = r[g * P * PACK + t : (g + 1) * P * PACK : PACK, :]
+            width = FEATS // pieces
+            for a in range(pieces):
+                piece = keep.tile([P, width], BF16, name="raw%d_%d" % (s, a))
+                nc.sync.dma_start(out=piece[:], in_=rows[:, a * width : (a + 1) * width])
+                words = piece[:].bitcast(F32)
+                for k in range(PASSES // pieces):
+                    raw[s, a * (PASSES // pieces) + k] = words[:, 256 * k : 256 * (k + 1)]
+
+        def load_words(h, a):
+            piece = keep.tile([P, 2, N], U32, name="g_words%d_%d" % (h, a), align_bytes=64)
+            nc.sync.dma_start(out=piece[:].bitcast(I32), in_=words_hbm[:, 2 * a : 2 * a + 2, h * N : (h + 1) * N])
+            for k in range(2):
+                g_words[h, 2 * a + k] = piece[:, k, :]
+
+        def load_scales(h):
+            for quad in range(4):
+                nc.sync.dma_start(
+                    out=g_scales[h][32 * quad : 32 * quad + 4, :, :].bitcast(I32),
+                    in_=q_scales[:, 4 * quad : 4 * quad + 4, h * N : (h + 1) * N].rearrange("g r n -> r g n").bitcast(I32),
+                )
+
+        nc.sync.dma_start(out=q_cols[:], in_=q_self.rearrange("(p c) -> p c", c=8))
+        load_slot(0, 2)
+        load_slot(1, 1)
+        load_scales(0)
+        load_slot(2, 1)
+        load_words(0, 0)
+        load_words(0, 1)
+        nc.sync.dma_start(out=r_cols[:], in_=r_self.rearrange("(g p t) -> p g t", p=P, t=PACK))
+        nc.sync.dma_start(out=gain_cols[:], in_=gain.rearrange("(g p t) -> p g t", p=P, t=PACK))
+        load_slot(3, 1)
+        load_slot(4, 1)
+        load_slot(5, 1)
+        load_scales(1)
+        load_words(1, 0)
+        load_words(1, 1)
+        for s in range(6, SLOTS):
+            load_slot(s, 1)
+
+        r_banks, r_grouped, r_codes, r_scales = {}, {}, {}, {}
+        acc, minus_union, inv_root, inv_union = {}, {}, {}, {}
+        y_sets, y_banks, y_grouped, y_codes, y_scales = {}, {}, {}, {}, {}
+
+        def copy_on(engine, out, in_):
+            if engine == "scalar":
+                nc.scalar.copy(out, in_)
+            else:
+                nc.vector.tensor_copy(out, in_)
+
+        def turn_slot(s):
+            for a in range(2):
+                bank = tr_psum.tile([P, 2, 2, P], F32, name="r_bank%d_%d" % (s, a), tag="turn")
+                for k in range(2):
+                    for u in range(2):
+                        nc.tensor.transpose(bank[:, k, u, :], raw[s, 2 * a + k][:, u::2], ident[:])
+                r_banks[s, a] = bank
+
+        def empty_slot(s, a, engine):
+            if a == 0:
+                r_grouped[s] = work.tile([P, FEATS], BF16, name="r_grouped%d" % s, tag="r_grouped", align_bytes=64)
+            words = r_grouped[s][:].bitcast(F32)[:, a * N : (a + 1) * N]
+            copy_on(
+                engine,
+                words.rearrange("p (k m u) -> p k m u", k=2, u=2),
+                r_banks[s, a][:].rearrange("p k u m -> p k m u"),
+            )
+
+        def quantize_slot(s):
+            r_codes[s] = keep.tile([P, PASSES * P], U32, name="r_codes%d" % s, align_bytes=64)
+            r_scales[s] = keep.tile([P, PASSES * P], U8, name="r_scales%d" % s, align_bytes=64)
+            nc.vector.quantize_mx(out=r_codes[s][:].bitcast(E4M3X4), scales=r_scales[s][:], in_=r_grouped[s][:])
+
+        def place(n):
+            e, t = divmod(n, PACK)
+            g, h = divmod(e, HALVES)
+            return e, g, h, t
+
+        def multiply(n):
+            e, g, h, t = place(n)
+            s = g * PACK + t
+            acc[n] = mx_psum.tile([P, N], F32, name="acc%d" % n, tag="acc")
+            for k in range(PASSES):
+                nc.tensor.matmul_mx(
+                    out=acc[n][:],
+                    lhsT=r_codes[s][:, k * P : (k + 1) * P].bitcast(E4M3X4),
+                    lhsT_scale=r_scales[s][:, k * P : (k + 1) * P],
+                    rhs=g_words[h, k].bitcast(E5M2X4),
+                    rhs_scale=g_scales[h][:, k, :],
+                    start=(k == 0),
+                    stop=(k == PASSES - 1),
+                )
+
+        def subtract(n, cols=slice(0, N)):
+            e, g, h, t = place(n)
+            if cols.start == 0:
+                minus_union[n] = work.tile([P, N], F32, name="minus_union%d" % n, tag="minus_union")
+            nc.vector.scalar_tensor_tensor(
+                out=minus_union[n][:, cols], in0=acc[n][:, cols], scalar=r_cols[:, g, t : t + 1],
+                in1=q_rows[:, h * N : (h + 1) * N][:, cols], op0=ALU.subtract, op1=ALU.subtract,
+            )
+
+        def root(n, cols=slice(0, N)):
+            if cols.start == 0:
+                inv_root[n] = work.tile([P, N], F32, name="inv_root%d" % n, tag="inv_root")
+            nc.scalar.activation(inv_root[n][:, cols], minus_union[n][:, cols], ACT.Abs_reciprocal_sqrt)
+
+        def square(n, cols=slice(0, N)):
+            if cols.start == 0:
+                inv_union[n] = work.tile([P, N], F32, name="inv_union%d" % n, tag="inv_union")
+            nc.scalar.activation(inv_union[n][:, cols], inv_root[n][:, cols], ACT.Square)
+
+        def finish(n, cols=slice(0, N)):
+            e, g, h, t = place(n)
+            if t == 0 and cols.start == 0:
+                y_sets[e] = work.tile([P, PACK, N], F32, name="y_set%d" % e, tag="y_set")
+            nc.vector.scalar_tensor_tensor(
+                out=y_sets[e][:, t, cols], in0=acc[n][:, cols], scalar=gain_cols[:, g, t : t + 1],
+                in1=inv_union[n][:, cols], op0=ALU.mult, op1=ALU.mult,
+            )
+
+        def turn_y(e, b, slots=range(PACK), pool=tr_psum, tag="turn"):
+            if slots.start == 0:
+                y_banks[e, b] = pool.tile([P, PACK, P], F32, name="y_bank%d_%d" % (e, b), tag=tag)
+            for t in slots:
+                nc.tensor.transpose(y_banks[e, b][:, t, :], y_sets[e][:, t, b * P : (b + 1) * P], ident[:])
+
+        def store_y(e, b, engine):
+            g, h = divmod(e, HALVES)
+            rows = work.tile([P, P, PACK], F32, name="y_rows%d_%d" % (e, b), tag="y_rows", bufs=8)
+            copy_on(engine, rows[:], y_banks[e, b][:].rearrange("i t p -> i p t"))
+            i0 = h * N + b * P
+            nc.sync.dma_start(out=out_0[i0 : i0 + P, g * N : (g + 1) * N], in_=rows[:].rearrange("i p t -> i (p t)"))
+
+        def round_y(e, a):
+            y_grouped[e, a] = work.tile([P, 256, PACK], BF16, name="y_grouped%d_%d" % (e, a), tag="y_grouped", align_bytes=64)
+            nc.vector.tensor_copy(
+                y_grouped[e, a][:].rearrange("p (c i) t -> p c t i", i=4),
+                y_sets[e][:, :, a * 256 : (a + 1) * 256].rearrange("p t (c i) -> p c t i", i=4),
+            )
+
+        def quantize_y(e, a):
+            g, h = divmod(e, HALVES)
+            if a == 0:
+                y_codes[e] = work.tile([P, N], U32, name="y_codes%d" % e, tag="y_codes", align_bytes=64)
+            if a == 0 and h == 0:
+                y_scales[g] = keep.tile([P, QUERIES], U8, name="y_scales%d" % g, align_bytes=64)
+            c0 = h * N + a * 256
+            nc.vector.quantize_mx(
+                out=y_codes[e][:, a * 256 : (a + 1) * 256].bitcast(E4M3X4),
+                scales=y_scales[g][:, c0 : c0 + 256],
+                in_=y_grouped[e, a][:].rearrange("p i t -> p (i t)"),
+            )
+            if a == 1:
+                codes_hbm = out_1[g].rearrange("p n t -> p (n t)").bitcast(I32)
+                nc.sync.dma_start(out=codes_hbm[:, h * N : (h + 1) * N], in_=y_codes[e][:].bitcast(I32))
+            if a == 1 and h == HALVES - 1:
+                for quad in range(4):
+                    nc.sync.dma_start(
+                        out=out_2[g, 4 * quad : 4 * quad + 4, :].bitcast(I32),
+                        in_=y_scales[g][32 * quad : 32 * quad + 4, :].bitcast(I32),
+                    )
+
+        turn_slot(0)
+        empty_slot(0, 0, "scalar")
+        empty_slot(0, 1, "vector")
+        nc.vector.tensor_copy(q_cols32[:], q_cols[:])
+        quantize_slot(0)
+        for a in range(2):
+            bank = tr_psum.tile([P, PACK, P], F32, name="q_bank%d" % a, tag="turn")
+            for c in range(PACK):
+                column = q_cols32[:, PACK * a + c : PACK * a + c + 1]
+                nc.tensor.transpose(bank[:, c, :], column.to_broadcast([P, P]), ident[:])
+            nc.scalar.copy(
+                q_rows[:].rearrange("p (n c) -> p n c", c=8)[:, :, PACK * a : PACK * a + PACK],
+                bank[:].rearrange("p c n -> p n c"),
+            )
+        turn_slot(1)
+        empty_slot(1, 0, "scalar")
+        empty_slot(1, 1, "vector")
+        turn_slot(2)
+        empty_slot(2, 0, "scalar")
+        quantize_slot(1)
+        empty_slot(2, 1, "scalar")
+
+        multiply(0)
+        multiply(1)
+        quantize_slot(2)
+        subtract(0)
+        root(0)
+        subtract(1)
+        turn_slot(3)
+        turn_slot(4)
+        square(0)
+        empty_slot(3, 0, "vector")
+        empty_slot(3, 1, "scalar")
+        multiply(2)
+        root(1)
+        finish(0)
+        quantize_slot(3)
+        multiply(3)
+        empty_slot(4, 0, "scalar")
+        square(1)
+        subtract(2)
+        empty_slot(4, 1, "scalar")
+        finish(1)
+        root(2)
+        subtract(3)
+        quantize_slot(4)
+        square(2)
+        turn_slot(5)
+
+        for c in range(2, 9):
+            first, second = 2 * c, 2 * c + 1
+            e, a = divmod(c - 2, 2)
+            pe, pa = divmod(c - 3, 2)
+            s = c + 4
+            vector_empties = c % 2 == 1
+            multiply(first)
+            multiply(second)
+            root(first - 1)
+            if c > 2:
+                round_y(pe, pa)
+                if vector_empties:
+                    store_y(pe, 2 * pa + 1, "vector")
+            finish(first - 2)
+            empty_slot(s - 1, 0, "scalar")
+            if c > 2:
+                quantize_y(pe, pa)
+            square(first - 1)
+            subtract(first)
+            finish(first - 1)
+            empty_slot(s - 1, 1, "scalar")
+            if c > 2:
+                store_y(pe, 2 * pa, "scalar")
+            root(first)
+            if c > 2 and not vector_empties:
+                store_y(pe, 2 * pa + 1, "scalar")
+            subtract(second)
+            square(first)
+            quantize_slot(s - 1)
+            if s < SLOTS:
+                turn_slot(s)
+                turn_y(e, 2 * a)
+                turn_y(e, 2 * a + 1)
+            else:
+                for b in range(PACK):
+                    turn_y(e, b)
+
+        for c in range(9, 12):
+            first, second = 2 * c, 2 * c + 1
+            pe, pa = divmod(c - 3, 2)
+            multiply(first)
+            multiply(second)
+            root(first - 1)
+            round_y(pe, pa)
+            store_y(pe, 2 * pa, "scalar")
+            finish(first - 2)
+            square(first - 1)
+            subtract(first)
+            store_y(pe, 2 * pa + 1, "scalar")
+            quantize_y(pe, pa)
+            finish(first - 1)
+            root(first)
+            if c < 11:
+                subtract(second)
+                square(first)
+            if c == 10:
+                for b in range(PACK):
+                    turn_y(SETS - 2, b)
+
+        e, last = SETS - 1, UNITS - 1
+        left, right = slice(0, 256), slice(256, N)
+        subtract(last, left)
+        subtract(last, right)
+        store_y(e - 1, 2, "scalar")
+        square(last - 1)
+        root(last, left)
+        root(last, right)
+        round_y(e - 1, 1)
+        finish(last - 1)
+        square(last, left)
+        square(last, right)
+        store_y(e - 1, 3, "scalar")
+        for b in range(PACK):
+            turn_y(e, b, range(0, 3))
+        finish(last, left)
+        finish(last, right)
+        for b in range(PACK):
+            turn_y(e, b, range(3, 4))
+        quantize_y(e - 1, 1)
+        round_y(e, 0)
+        store_y(e, 0, "scalar")
+        store_y(e, 2, "vector")
+        store_y(e, 1, "scalar")
+        round_y(e, 1)
+        store_y(e, 3, "scalar")
+        quantize_y(e, 0)
+        quantize_y(e, 1)

@@ -19,12 +19,36 @@ ACT = mybir.ActivationFunctionType
 P = 128
 PACK = 4
 N = 512
+QUADS = 4
 PASSES = FEATS // (P * PACK)
 GROUPS = REFS // (P * PACK)
 HALVES = QUERIES // N
 SLOTS = GROUPS * PACK
-UNITS = GROUPS * HALVES * PACK
 SETS = GROUPS * HALVES
+UNITS = SETS * PACK
+
+WHOLE, LEFT, RIGHT = slice(0, N), slice(0, N // 2), slice(N // 2, N)
+
+SLOT_LEAD = 4
+LATE_UNIT = 2 * (SLOTS - SLOT_LEAD + 1)
+FIRST_SHARED_SLOT = 2 + SLOT_LEAD
+
+R_BANK, Y_BANK = 4, 6
+
+
+def slot_bank(s, a):
+    banks = 4 if s < FIRST_SHARED_SLOT else 2
+    return R_BANK + (2 * s + a) % banks
+
+
+def unit_bank(n):
+    return n % R_BANK if n < LATE_UNIT else (n - LATE_UNIT + R_BANK) % Y_BANK
+
+
+def place(n):
+    e, t = divmod(n, PACK)
+    g, h = divmod(e, HALVES)
+    return e, g, h, t
 
 
 def tile_tanimoto_weighted_similarity_planes_k2_kernel(
@@ -34,29 +58,34 @@ def tile_tanimoto_weighted_similarity_planes_k2_kernel(
     with ExitStack() as ctx:
         keep = ctx.enter_context(tc.tile_pool(name="keep", bufs=1))
         work = ctx.enter_context(tc.tile_pool(name="work", bufs=3))
-        mx_psum = ctx.enter_context(tc.psum_pool(name="mx_psum", bufs=4))
-        tr_psum = ctx.enter_context(tc.psum_pool(name="tr_psum", bufs=4))
+        psum = ctx.enter_context(tc.psum_pool(name="psum", bufs=1))
         ctx.enter_context(tc.manual_schedule())
 
         ident = keep.tile([P, P], F32, name="ident")
         g_scales = [keep.tile([P, PASSES, N], U8, name="g_scales%d" % h, align_bytes=64) for h in range(HALVES)]
-        q_cols = keep.tile([P, 8], BF16, name="q_cols")
-        q_cols32 = keep.tile([P, 8], F32, name="q_cols32")
-        q_rows = keep.tile([P, QUERIES], F32, name="q_rows")
-        r_cols = keep.tile([P, GROUPS, PACK], BF16, name="r_cols")
-        gain_cols = keep.tile([P, GROUPS, PACK], BF16, name="gain_cols")
-        warm = keep.tile([P, 1], F32, name="warm")
-        warm_out = keep.tile([P, 1], F32, name="warm_out")
+        q_cols = keep.tile([P, HALVES, PACK], BF16, name="q_cols")
+        q_cols32 = keep.tile([P, HALVES, PACK], F32, name="q_cols32")
+        q_rows = [keep.tile([P, N], F32, name="q_rows%d" % h) for h in range(HALVES)]
+        r_cols = keep.tile([P, SLOTS], BF16, name="r_cols")
+        gain_cols = keep.tile([P, SLOTS], BF16, name="gain_cols")
+        gain_root = keep.tile([P, SLOTS], F32, name="gain_root")
+        gain_guess = keep.tile([P, SLOTS], F32, name="gain_guess")
+        gain_check = keep.tile([P, SLOTS], F32, name="gain_check")
+        inv_gain = keep.tile([P, SLOTS], F32, name="inv_gain")
+        r_over_gain = keep.tile([P, SLOTS], F32, name="r_over_gain")
 
-        nc.vector.memset(warm[:], 1.0)
         for h in range(HALVES):
             nc.vector.memset(g_scales[h][:].rearrange("p g n -> p (g n)").bitcast(I32), 0)
-        nc.scalar.activation(warm_out[:], warm[:], ACT.Abs_reciprocal_sqrt)
         make_identity(nc, ident[:])
 
-        raw = {}
-        g_words = {}
+        raw, g_words = {}, {}
         words_hbm = q_words.rearrange("g p n t -> p g (n t)").bitcast(I32)
+
+        def load_by_slot(cols, vector):
+            nc.sync.dma_start(
+                out=cols[:].rearrange("p (g t) -> p g t", t=PACK),
+                in_=vector.rearrange("(g p t) -> p g t", p=P, t=PACK),
+            )
 
         def load_slot(s, pieces):
             g, t = divmod(s, PACK)
@@ -66,8 +95,8 @@ def tile_tanimoto_weighted_similarity_planes_k2_kernel(
                 piece = keep.tile([P, width], BF16, name="raw%d_%d" % (s, a))
                 nc.sync.dma_start(out=piece[:], in_=rows[:, a * width : (a + 1) * width])
                 words = piece[:].bitcast(F32)
-                for k in range(PASSES // pieces):
-                    raw[s, a * (PASSES // pieces) + k] = words[:, 256 * k : 256 * (k + 1)]
+                for b in range(2 // pieces):
+                    raw[s, a + b] = words[:, N * b : N * (b + 1)]
 
         def load_words(h, a):
             piece = keep.tile([P, 2, N], U32, name="g_words%d_%d" % (h, a), align_bytes=64)
@@ -76,32 +105,32 @@ def tile_tanimoto_weighted_similarity_planes_k2_kernel(
                 g_words[h, 2 * a + k] = piece[:, k, :]
 
         def load_scales(h):
-            for quad in range(4):
+            for quad in range(QUADS):
+                rows = q_scales[:, 4 * quad : 4 * quad + 4, h * N : (h + 1) * N]
                 nc.sync.dma_start(
                     out=g_scales[h][32 * quad : 32 * quad + 4, :, :].bitcast(I32),
-                    in_=q_scales[:, 4 * quad : 4 * quad + 4, h * N : (h + 1) * N].rearrange("g r n -> r g n").bitcast(I32),
+                    in_=rows.rearrange("g r n -> r g n").bitcast(I32),
                 )
 
-        nc.sync.dma_start(out=q_cols[:], in_=q_self.rearrange("(p c) -> p c", c=8))
+        load_by_slot(gain_cols, gain)
         load_slot(0, 2)
+        nc.sync.dma_start(out=q_cols[:], in_=q_self.rearrange("(h p c) -> p h c", p=P, c=PACK))
         load_slot(1, 1)
         load_scales(0)
-        load_slot(2, 1)
         load_words(0, 0)
+        load_slot(2, 1)
         load_words(0, 1)
-        nc.sync.dma_start(out=r_cols[:], in_=r_self.rearrange("(g p t) -> p g t", p=P, t=PACK))
-        nc.sync.dma_start(out=gain_cols[:], in_=gain.rearrange("(g p t) -> p g t", p=P, t=PACK))
-        load_slot(3, 1)
-        load_slot(4, 1)
-        load_slot(5, 1)
+        load_by_slot(r_cols, r_self)
+        for s in range(3, FIRST_SHARED_SLOT):
+            load_slot(s, 1)
         load_scales(1)
         load_words(1, 0)
         load_words(1, 1)
-        for s in range(6, SLOTS):
+        for s in range(FIRST_SHARED_SLOT, SLOTS):
             load_slot(s, 1)
 
-        r_banks, r_grouped, r_codes, r_scales = {}, {}, {}, {}
-        acc, minus_union, inv_root, inv_union = {}, {}, {}, {}
+        r_sorted, r_banks, r_grouped, r_codes, r_scales = {}, {}, {}, {}, {}
+        inter, q_less_inter, inv_root, gain_over_union = {}, {}, {}, {}
         y_sets, y_banks, y_grouped, y_codes, y_scales = {}, {}, {}, {}, {}
 
         def copy_on(engine, out, in_):
@@ -110,15 +139,24 @@ def tile_tanimoto_weighted_similarity_planes_k2_kernel(
             else:
                 nc.vector.tensor_copy(out, in_)
 
+
+        def sort_half(s, a):
+            r_sorted[s, a] = work.tile([P, 2, 2, P], F32, name="r_sorted%d_%d" % (s, a), tag="r_sorted", bufs=4)
+            nc.vector.tensor_copy(r_sorted[s, a][:], raw[s, a].rearrange("m (k p u) -> m k u p", k=2, u=2))
+
         def turn_slot(s):
             for a in range(2):
-                bank = tr_psum.tile([P, 2, 2, P], F32, name="r_bank%d_%d" % (s, a), tag="turn")
+                bank = psum.tile([P, 2, 2, P], F32, name="r_bank%d_%d" % (s, a), tag="bank%d" % slot_bank(s, a))
                 for k in range(2):
                     for u in range(2):
-                        nc.tensor.transpose(bank[:, k, u, :], raw[s, 2 * a + k][:, u::2], ident[:])
+                        if (s, a) in r_sorted:
+                            words = r_sorted[s, a][:, k, u, :]
+                        else:
+                            words = raw[s, a][:, 2 * P * k + u : 2 * P * (k + 1) : 2]
+                        nc.tensor.transpose(bank[:, k, u, :], words, ident[:])
                 r_banks[s, a] = bank
 
-        def empty_slot(s, a, engine):
+        def empty_half(s, a, engine):
             if a == 0:
                 r_grouped[s] = work.tile([P, FEATS], BF16, name="r_grouped%d" % s, tag="r_grouped", align_bytes=64)
             words = r_grouped[s][:].bitcast(F32)[:, a * N : (a + 1) * N]
@@ -128,23 +166,31 @@ def tile_tanimoto_weighted_similarity_planes_k2_kernel(
                 r_banks[s, a][:].rearrange("p k u m -> p k m u"),
             )
 
-        def quantize_slot(s):
-            r_codes[s] = keep.tile([P, PASSES * P], U32, name="r_codes%d" % s, align_bytes=64)
-            r_scales[s] = keep.tile([P, PASSES * P], U8, name="r_scales%d" % s, align_bytes=64)
-            nc.vector.quantize_mx(out=r_codes[s][:].bitcast(E4M3X4), scales=r_scales[s][:], in_=r_grouped[s][:])
+        def quantize_slot(s, cols=WHOLE):
+            if cols.start == 0:
+                r_codes[s] = keep.tile([P, PASSES * P], U32, name="r_codes%d" % s, align_bytes=64)
+                r_scales[s] = keep.tile([P, PASSES * P], U8, name="r_scales%d" % s, align_bytes=64)
+            nc.vector.quantize_mx(
+                out=r_codes[s][:, cols].bitcast(E4M3X4),
+                scales=r_scales[s][:, cols],
+                in_=r_grouped[s][:, PACK * cols.start : PACK * cols.stop],
+            )
 
-        def place(n):
-            e, t = divmod(n, PACK)
-            g, h = divmod(e, HALVES)
-            return e, g, h, t
+        def spread_q(h):
+            bank = psum.tile([P, PACK, P], F32, name="q_bank%d" % h, tag="bank%d" % unit_bank(PACK - 1 - h))
+            for c in range(PACK):
+                nc.tensor.transpose(bank[:, c, :], q_cols32[:, h, c : c + 1].to_broadcast([P, P]), ident[:])
+            nc.scalar.copy(q_rows[h][:].rearrange("p (n c) -> p n c", c=PACK), bank[:].rearrange("p c n -> p n c"))
 
-        def multiply(n):
+
+        def multiply(n, passes=range(PASSES)):
             e, g, h, t = place(n)
             s = g * PACK + t
-            acc[n] = mx_psum.tile([P, N], F32, name="acc%d" % n, tag="acc")
-            for k in range(PASSES):
+            if passes.start == 0:
+                inter[n] = psum.tile([P, N], F32, name="inter%d" % n, tag="bank%d" % unit_bank(n))
+            for k in passes:
                 nc.tensor.matmul_mx(
-                    out=acc[n][:],
+                    out=inter[n][:],
                     lhsT=r_codes[s][:, k * P : (k + 1) * P].bitcast(E4M3X4),
                     lhsT_scale=r_scales[s][:, k * P : (k + 1) * P],
                     rhs=g_words[h, k].bitcast(E5M2X4),
@@ -153,37 +199,44 @@ def tile_tanimoto_weighted_similarity_planes_k2_kernel(
                     stop=(k == PASSES - 1),
                 )
 
-        def subtract(n, cols=slice(0, N)):
+        def subtract(n, cols=WHOLE):
             e, g, h, t = place(n)
             if cols.start == 0:
-                minus_union[n] = work.tile([P, N], F32, name="minus_union%d" % n, tag="minus_union")
-            nc.vector.scalar_tensor_tensor(
-                out=minus_union[n][:, cols], in0=acc[n][:, cols], scalar=r_cols[:, g, t : t + 1],
-                in1=q_rows[:, h * N : (h + 1) * N][:, cols], op0=ALU.subtract, op1=ALU.subtract,
+                q_less_inter[n] = work.tile([P, N], F32, name="q_less_inter%d" % n, tag="q_less_inter")
+            nc.vector.tensor_tensor(
+                out=q_less_inter[n][:, cols], in0=q_rows[h][:, cols], in1=inter[n][:, cols], op=ALU.subtract
             )
 
-        def root(n, cols=slice(0, N)):
+        def root(n, cols=WHOLE):
+            e, g, h, t = place(n)
+            s = g * PACK + t
             if cols.start == 0:
                 inv_root[n] = work.tile([P, N], F32, name="inv_root%d" % n, tag="inv_root")
-            nc.scalar.activation(inv_root[n][:, cols], minus_union[n][:, cols], ACT.Abs_reciprocal_sqrt)
+            nc.scalar.activation(
+                inv_root[n][:, cols],
+                q_less_inter[n][:, cols],
+                ACT.Abs_reciprocal_sqrt,
+                bias=r_over_gain[:, s : s + 1],
+                scale=inv_gain[:, s : s + 1],
+            )
 
-        def square(n, cols=slice(0, N)):
+        def square(n, cols=WHOLE):
             if cols.start == 0:
-                inv_union[n] = work.tile([P, N], F32, name="inv_union%d" % n, tag="inv_union")
-            nc.scalar.activation(inv_union[n][:, cols], inv_root[n][:, cols], ACT.Square)
+                gain_over_union[n] = work.tile([P, N], F32, name="gain_over_union%d" % n, tag="gain_over_union")
+            nc.scalar.activation(gain_over_union[n][:, cols], inv_root[n][:, cols], ACT.Square)
 
-        def finish(n, cols=slice(0, N)):
+        def finish(n, cols=WHOLE):
             e, g, h, t = place(n)
             if t == 0 and cols.start == 0:
                 y_sets[e] = work.tile([P, PACK, N], F32, name="y_set%d" % e, tag="y_set")
-            nc.vector.scalar_tensor_tensor(
-                out=y_sets[e][:, t, cols], in0=acc[n][:, cols], scalar=gain_cols[:, g, t : t + 1],
-                in1=inv_union[n][:, cols], op0=ALU.mult, op1=ALU.mult,
+            nc.vector.tensor_tensor(
+                out=y_sets[e][:, t, cols], in0=inter[n][:, cols], in1=gain_over_union[n][:, cols], op=ALU.mult
             )
 
-        def turn_y(e, b, slots=range(PACK), pool=tr_psum, tag="turn"):
+
+        def turn_y(e, b, bank, slots=range(PACK)):
             if slots.start == 0:
-                y_banks[e, b] = pool.tile([P, PACK, P], F32, name="y_bank%d_%d" % (e, b), tag=tag)
+                y_banks[e, b] = psum.tile([P, PACK, P], F32, name="y_bank%d_%d" % (e, b), tag="bank%d" % bank)
             for t in slots:
                 nc.tensor.transpose(y_banks[e, b][:, t, :], y_sets[e][:, t, b * P : (b + 1) * P], ident[:])
 
@@ -194,11 +247,21 @@ def tile_tanimoto_weighted_similarity_planes_k2_kernel(
             i0 = h * N + b * P
             nc.sync.dma_start(out=out_0[i0 : i0 + P, g * N : (g + 1) * N], in_=rows[:].rearrange("i p t -> i (p t)"))
 
-        def round_y(e, a):
-            y_grouped[e, a] = work.tile([P, 256, PACK], BF16, name="y_grouped%d_%d" % (e, a), tag="y_grouped", align_bytes=64)
+        def round_on_gpsimd(e, a):
+            y_grouped[e, a] = work.tile(
+                [P, N // 2, PACK], BF16, name="y_grouped%d_%d" % (e, a), tag="y_gpsimd", bufs=1, align_bytes=64
+            )
+            part = y_sets[e][:, :, (LEFT, RIGHT)[a]]
+            nc.gpsimd.tensor_scalar(y_grouped[e, a][:], part.rearrange("p t i -> p i t"), 1.0, 0.0, ALU.mult, ALU.add)
+
+        def round_on_vector(e, a):
+            y_grouped[e, a] = work.tile(
+                [P, N // 2, PACK], BF16, name="y_grouped%d_%d" % (e, a), tag="y_vector", bufs=2, align_bytes=64
+            )
+            part = y_sets[e][:, :, (LEFT, RIGHT)[a]]
             nc.vector.tensor_copy(
                 y_grouped[e, a][:].rearrange("p (c i) t -> p c t i", i=4),
-                y_sets[e][:, :, a * 256 : (a + 1) * 256].rearrange("p t (c i) -> p c t i", i=4),
+                part.rearrange("p t (c i) -> p c t i", i=4),
             )
 
         def quantize_y(e, a):
@@ -207,155 +270,166 @@ def tile_tanimoto_weighted_similarity_planes_k2_kernel(
                 y_codes[e] = work.tile([P, N], U32, name="y_codes%d" % e, tag="y_codes", align_bytes=64)
             if a == 0 and h == 0:
                 y_scales[g] = keep.tile([P, QUERIES], U8, name="y_scales%d" % g, align_bytes=64)
-            c0 = h * N + a * 256
+            cols = (LEFT, RIGHT)[a]
             nc.vector.quantize_mx(
-                out=y_codes[e][:, a * 256 : (a + 1) * 256].bitcast(E4M3X4),
-                scales=y_scales[g][:, c0 : c0 + 256],
+                out=y_codes[e][:, cols].bitcast(E4M3X4),
+                scales=y_scales[g][:, h * N + cols.start : h * N + cols.stop],
                 in_=y_grouped[e, a][:].rearrange("p i t -> p (i t)"),
             )
             if a == 1:
                 codes_hbm = out_1[g].rearrange("p n t -> p (n t)").bitcast(I32)
                 nc.sync.dma_start(out=codes_hbm[:, h * N : (h + 1) * N], in_=y_codes[e][:].bitcast(I32))
             if a == 1 and h == HALVES - 1:
-                for quad in range(4):
+                for quad in range(QUADS):
                     nc.sync.dma_start(
                         out=out_2[g, 4 * quad : 4 * quad + 4, :].bitcast(I32),
                         in_=y_scales[g][32 * quad : 32 * quad + 4, :].bitcast(I32),
                     )
 
+        nc.scalar.activation(gain_root[:], gain_cols[:], ACT.Abs_reciprocal_sqrt)
+        nc.scalar.activation(gain_guess[:], gain_root[:], ACT.Square)
+        sort_half(0, 0)
+        sort_half(0, 1)
         turn_slot(0)
-        empty_slot(0, 0, "scalar")
-        empty_slot(0, 1, "vector")
+        empty_half(0, 0, "scalar")
+        empty_half(0, 1, "scalar")
         nc.vector.tensor_copy(q_cols32[:], q_cols[:])
-        quantize_slot(0)
-        for a in range(2):
-            bank = tr_psum.tile([P, PACK, P], F32, name="q_bank%d" % a, tag="turn")
-            for c in range(PACK):
-                column = q_cols32[:, PACK * a + c : PACK * a + c + 1]
-                nc.tensor.transpose(bank[:, c, :], column.to_broadcast([P, P]), ident[:])
-            nc.scalar.copy(
-                q_rows[:].rearrange("p (n c) -> p n c", c=8)[:, :, PACK * a : PACK * a + PACK],
-                bank[:].rearrange("p c n -> p n c"),
-            )
+        sort_half(1, 0)
+        sort_half(1, 1)
         turn_slot(1)
-        empty_slot(1, 0, "scalar")
-        empty_slot(1, 1, "vector")
-        turn_slot(2)
-        empty_slot(2, 0, "scalar")
+        quantize_slot(0, LEFT)
+        nc.vector.scalar_tensor_tensor(
+            out=gain_check[:], in0=gain_guess[:], scalar=-1.0, in1=gain_cols[:], op0=ALU.mult, op1=ALU.mult
+        )
+        quantize_slot(0, RIGHT)
+        nc.vector.scalar_tensor_tensor(
+            out=inv_gain[:], in0=gain_check[:], scalar=2.0, in1=gain_guess[:], op0=ALU.add, op1=ALU.mult
+        )
+        empty_half(1, 0, "scalar")
+        empty_half(1, 1, "vector")
+        spread_q(0)
         quantize_slot(1)
-        empty_slot(2, 1, "scalar")
 
-        multiply(0)
+        multiply(0, range(0, 2))
+        spread_q(1)
+        sort_half(2, 1)
+        turn_slot(2)
+        multiply(0, range(2, PASSES))
         multiply(1)
-        quantize_slot(2)
+        empty_half(2, 0, "scalar")
+        empty_half(2, 1, "vector")
+        nc.vector.tensor_tensor(out=r_over_gain[:], in0=r_cols[:], in1=inv_gain[:], op=ALU.mult)
         subtract(0)
+        quantize_slot(2)
+        sort_half(3, 1)
+        turn_slot(3)
         root(0)
         subtract(1)
-        turn_slot(3)
-        turn_slot(4)
-        square(0)
-        empty_slot(3, 0, "vector")
-        empty_slot(3, 1, "scalar")
-        multiply(2)
-        root(1)
-        finish(0)
-        quantize_slot(3)
-        multiply(3)
-        empty_slot(4, 0, "scalar")
-        square(1)
-        subtract(2)
-        empty_slot(4, 1, "scalar")
-        finish(1)
-        root(2)
-        subtract(3)
-        quantize_slot(4)
-        square(2)
-        turn_slot(5)
+        sort_half(4, 1)
 
-        for c in range(2, 9):
+        for n in (2, 3):
+            multiply(n)
+            empty_half(n + 1, 0, "scalar")
+            empty_half(n + 1, 1, "scalar")
+            square(n - 2)
+            root(n - 1)
+            turn_slot(n + 2)
+            quantize_slot(n + 1)
+            subtract(n)
+            finish(n - 2)
+            sort_half(n + 3, 1)
+        square(2)
+
+        for c in range(2, LATE_UNIT // 2):
             first, second = 2 * c, 2 * c + 1
             e, a = divmod(c - 2, 2)
-            pe, pa = divmod(c - 3, 2)
-            s = c + 4
-            vector_empties = c % 2 == 1
+            old_e, old_a = divmod(c - 3, 2)
+            has_old = c > 2
+            s = c + SLOT_LEAD
             multiply(first)
             multiply(second)
+            if has_old:
+                store_y(old_e, 2 * old_a, "vector")
+            empty_half(s - 1, 0, "scalar")
             root(first - 1)
-            if c > 2:
-                round_y(pe, pa)
-                if vector_empties:
-                    store_y(pe, 2 * pa + 1, "vector")
             finish(first - 2)
-            empty_slot(s - 1, 0, "scalar")
-            if c > 2:
-                quantize_y(pe, pa)
-            square(first - 1)
+            empty_half(s - 1, 1, "scalar")
             subtract(first)
-            finish(first - 1)
-            empty_slot(s - 1, 1, "scalar")
-            if c > 2:
-                store_y(pe, 2 * pa, "scalar")
-            root(first)
-            if c > 2 and not vector_empties:
-                store_y(pe, 2 * pa + 1, "scalar")
-            subtract(second)
-            square(first)
+            square(first - 1)
             quantize_slot(s - 1)
+            finish(first - 1)
+            root(first)
+            if s + 1 < SLOTS and c % 2 == 0:
+                sort_half(s + 1, 1)
+            if has_old:
+                quantize_y(old_e, old_a)
+            round_on_gpsimd(e, a)
+            subtract(second)
+            if has_old:
+                store_y(old_e, 2 * old_a + 1, "scalar")
+            square(first)
             if s < SLOTS:
                 turn_slot(s)
-                turn_y(e, 2 * a)
-                turn_y(e, 2 * a + 1)
             else:
-                for b in range(PACK):
-                    turn_y(e, b)
+                multiply(LATE_UNIT)
+            turn_y(e, 2 * a, Y_BANK)
+            turn_y(e, 2 * a + 1, Y_BANK + 1)
 
-        for c in range(9, 12):
-            first, second = 2 * c, 2 * c + 1
-            pe, pa = divmod(c - 3, 2)
-            multiply(first)
-            multiply(second)
-            root(first - 1)
-            round_y(pe, pa)
-            store_y(pe, 2 * pa, "scalar")
-            finish(first - 2)
-            square(first - 1)
-            subtract(first)
-            store_y(pe, 2 * pa + 1, "scalar")
-            quantize_y(pe, pa)
-            finish(first - 1)
-            root(first)
-            if c < 11:
-                subtract(second)
-                square(first)
-            if c == 10:
+        last_set, last = SETS - 1, UNITS - 1
+        multiply(LATE_UNIT + 1)
+        for n in range(LATE_UNIT, last):
+            e, a = divmod(n // 2 - 3, 2)
+            root(n - 1)
+            subtract(n)
+            finish(n - 2)
+            if n + 2 < last:
+                multiply(n + 2)
+            if n % 2 == 0:
+                store_y(e, 2 * a + 1, "scalar")
+                store_y(e, 2 * a, "vector")
+            else:
+                quantize_y(e, a)
+                next_e, next_a = divmod(n // 2 - 2, 2)
+                round_on_gpsimd(next_e, next_a)
+            square(n - 1)
+            if n == LATE_UNIT:
+                turn_y(e, 2, Y_BANK)
+                turn_y(e, 3, Y_BANK + 1)
+            if n + 2 == last:
+                banks = (Y_BANK, Y_BANK + 1, unit_bank(n - 3), unit_bank(n - 2))
                 for b in range(PACK):
-                    turn_y(SETS - 2, b)
+                    if b == 2:
+                        multiply(last)
+                    turn_y(last_set - 1, b, banks[b])
 
-        e, last = SETS - 1, UNITS - 1
-        left, right = slice(0, 256), slice(256, N)
-        subtract(last, left)
-        subtract(last, right)
-        store_y(e - 1, 2, "scalar")
+        root(last - 1)
+        subtract(last, LEFT)
+        subtract(last, RIGHT)
+        quantize_y(last_set - 1, 0)
+        round_on_gpsimd(last_set - 1, 1)
+        finish(last - 2)
+        root(last, LEFT)
         square(last - 1)
-        root(last, left)
-        root(last, right)
-        round_y(e - 1, 1)
+        root(last, RIGHT)
+        store_y(last_set - 1, 2, "vector")
         finish(last - 1)
-        square(last, left)
-        square(last, right)
-        store_y(e - 1, 3, "scalar")
+        square(last, LEFT)
+        square(last, RIGHT)
+        store_y(last_set - 1, 3, "scalar")
+        banks = (unit_bank(last - 3), unit_bank(last - 2), Y_BANK, Y_BANK + 1)
+        for slots in (range(0, 2), range(2, 3)):
+            for b in range(PACK):
+                turn_y(last_set, b, banks[b], slots)
+        finish(last, LEFT)
+        finish(last, RIGHT)
         for b in range(PACK):
-            turn_y(e, b, range(0, 3))
-        finish(last, left)
-        finish(last, right)
-        for b in range(PACK):
-            turn_y(e, b, range(3, 4))
-        quantize_y(e - 1, 1)
-        round_y(e, 0)
-        store_y(e, 0, "scalar")
-        store_y(e, 2, "vector")
-        store_y(e, 1, "scalar")
-        round_y(e, 1)
-        store_y(e, 3, "scalar")
-        quantize_y(e, 0)
-        quantize_y(e, 1)
+            turn_y(last_set, b, banks[b], range(3, PACK))
+        quantize_y(last_set - 1, 1)
+        store_y(last_set, 0, "scalar")
+        round_on_vector(last_set, 0)
+        store_y(last_set, 1, "scalar")
+        round_on_vector(last_set, 1)
+        store_y(last_set, 2, "scalar")
+        quantize_y(last_set, 0)
+        quantize_y(last_set, 1)
+        store_y(last_set, 3, "scalar")

from contextlib import ExitStack

import concourse.mybir as mybir
from concourse.masks import make_identity

QUERIES, REFS, FEATS = 1024, 1536, 2048
FLOPS = 2 * QUERIES * REFS * FEATS

F32 = mybir.dt.float32
BF16 = mybir.dt.bfloat16
I32 = mybir.dt.int32
U32 = mybir.dt.uint32
U8 = mybir.dt.uint8
E4M3X4 = mybir.dt.float8_e4m3fn_x4
E5M2X4 = mybir.dt.float8_e5m2_x4
ALU = mybir.AluOpType
ACT = mybir.ActivationFunctionType

P = 128
PACK = 4
N = 512
QUADS = 4
PASSES = FEATS // (P * PACK)
GROUPS = REFS // (P * PACK)
HALVES = QUERIES // N
SLOTS = GROUPS * PACK
SETS = GROUPS * HALVES
UNITS = SETS * PACK

WHOLE, LEFT, RIGHT = slice(0, N), slice(0, N // 2), slice(N // 2, N)

SLOT_LEAD = 4
LATE_UNIT = 2 * (SLOTS - SLOT_LEAD + 1)
FIRST_SHARED_SLOT = 2 + SLOT_LEAD

R_BANK, Y_BANK = 4, 6


def slot_bank(s, a):
    banks = 4 if s < FIRST_SHARED_SLOT else 2
    return R_BANK + (2 * s + a) % banks


def unit_bank(n):
    return n % R_BANK if n < LATE_UNIT else (n - LATE_UNIT + R_BANK) % Y_BANK


def place(n):
    e, t = divmod(n, PACK)
    g, h = divmod(e, HALVES)
    return e, g, h, t


def tile_tanimoto_weighted_similarity_planes_k2_kernel(
    tc, q_words, q_scales, r, q_self, r_self, gain, out_0, out_1, out_2
):
    nc = tc.nc
    with ExitStack() as ctx:
        keep = ctx.enter_context(tc.tile_pool(name="keep", bufs=1))
        work = ctx.enter_context(tc.tile_pool(name="work", bufs=3))
        psum = ctx.enter_context(tc.psum_pool(name="psum", bufs=1))
        ctx.enter_context(tc.manual_schedule())

        ident = keep.tile([P, P], F32, name="ident")
        g_scales = [keep.tile([P, PASSES, N], U8, name="g_scales%d" % h, align_bytes=64) for h in range(HALVES)]
        q_cols = keep.tile([P, HALVES, PACK], BF16, name="q_cols")
        q_cols32 = keep.tile([P, HALVES, PACK], F32, name="q_cols32")
        q_rows = [keep.tile([P, N], F32, name="q_rows%d" % h) for h in range(HALVES)]
        r_cols = keep.tile([P, SLOTS], BF16, name="r_cols")
        gain_cols = keep.tile([P, SLOTS], BF16, name="gain_cols")
        gain_root = keep.tile([P, SLOTS], F32, name="gain_root")
        gain_guess = keep.tile([P, SLOTS], F32, name="gain_guess")
        gain_check = keep.tile([P, SLOTS], F32, name="gain_check")
        inv_gain = keep.tile([P, SLOTS], F32, name="inv_gain")
        r_over_gain = keep.tile([P, SLOTS], F32, name="r_over_gain")

        for h in range(HALVES):
            nc.vector.memset(g_scales[h][:].rearrange("p g n -> p (g n)").bitcast(I32), 0)
        make_identity(nc, ident[:])

        raw, g_words = {}, {}
        words_hbm = q_words.rearrange("g p n t -> p g (n t)").bitcast(I32)

        def load_by_slot(cols, vector):
            nc.sync.dma_start(
                out=cols[:].rearrange("p (g t) -> p g t", t=PACK),
                in_=vector.rearrange("(g p t) -> p g t", p=P, t=PACK),
            )

        def load_slot(s, pieces):
            g, t = divmod(s, PACK)
            rows = r[g * P * PACK + t : (g + 1) * P * PACK : PACK, :]
            width = FEATS // pieces
            for a in range(pieces):
                piece = keep.tile([P, width], BF16, name="raw%d_%d" % (s, a))
                nc.sync.dma_start(out=piece[:], in_=rows[:, a * width : (a + 1) * width])
                words = piece[:].bitcast(F32)
                for b in range(2 // pieces):
                    raw[s, a + b] = words[:, N * b : N * (b + 1)]

        def load_words(h, a):
            piece = keep.tile([P, 2, N], U32, name="g_words%d_%d" % (h, a), align_bytes=64)
            nc.sync.dma_start(out=piece[:].bitcast(I32), in_=words_hbm[:, 2 * a : 2 * a + 2, h * N : (h + 1) * N])
            for k in range(2):
                g_words[h, 2 * a + k] = piece[:, k, :]

        def load_scales(h):
            for quad in range(QUADS):
                rows = q_scales[:, 4 * quad : 4 * quad + 4, h * N : (h + 1) * N]
                nc.sync.dma_start(
                    out=g_scales[h][32 * quad : 32 * quad + 4, :, :].bitcast(I32),
                    in_=rows.rearrange("g r n -> r g n").bitcast(I32),
                )

        load_by_slot(gain_cols, gain)
        load_slot(0, 2)
        nc.sync.dma_start(out=q_cols[:], in_=q_self.rearrange("(h p c) -> p h c", p=P, c=PACK))
        load_slot(1, 1)
        load_scales(0)
        load_words(0, 0)
        load_slot(2, 1)
        load_words(0, 1)
        load_by_slot(r_cols, r_self)
        for s in range(3, FIRST_SHARED_SLOT):
            load_slot(s, 1)
        load_scales(1)
        load_words(1, 0)
        load_words(1, 1)
        for s in range(FIRST_SHARED_SLOT, SLOTS):
            load_slot(s, 1)

        r_sorted, r_banks, r_grouped, r_codes, r_scales = {}, {}, {}, {}, {}
        inter, q_less_inter, inv_root, gain_over_union = {}, {}, {}, {}
        y_sets, y_banks, y_grouped, y_codes, y_scales = {}, {}, {}, {}, {}

        def copy_on(engine, out, in_):
            if engine == "scalar":
                nc.scalar.copy(out, in_)
            else:
                nc.vector.tensor_copy(out, in_)


        def sort_half(s, a):
            r_sorted[s, a] = work.tile([P, 2, 2, P], F32, name="r_sorted%d_%d" % (s, a), tag="r_sorted", bufs=4)
            nc.vector.tensor_copy(r_sorted[s, a][:], raw[s, a].rearrange("m (k p u) -> m k u p", k=2, u=2))

        def turn_slot(s):
            for a in range(2):
                bank = psum.tile([P, 2, 2, P], F32, name="r_bank%d_%d" % (s, a), tag="bank%d" % slot_bank(s, a))
                for k in range(2):
                    for u in range(2):
                        if (s, a) in r_sorted:
                            words = r_sorted[s, a][:, k, u, :]
                        else:
                            words = raw[s, a][:, 2 * P * k + u : 2 * P * (k + 1) : 2]
                        nc.tensor.transpose(bank[:, k, u, :], words, ident[:])
                r_banks[s, a] = bank

        def empty_half(s, a, engine):
            if a == 0:
                r_grouped[s] = work.tile([P, FEATS], BF16, name="r_grouped%d" % s, tag="r_grouped", align_bytes=64)
            words = r_grouped[s][:].bitcast(F32)[:, a * N : (a + 1) * N]
            copy_on(
                engine,
                words.rearrange("p (k m u) -> p k m u", k=2, u=2),
                r_banks[s, a][:].rearrange("p k u m -> p k m u"),
            )

        def quantize_slot(s, cols=WHOLE):
            if cols.start == 0:
                r_codes[s] = keep.tile([P, PASSES * P], U32, name="r_codes%d" % s, align_bytes=64)
                r_scales[s] = keep.tile([P, PASSES * P], U8, name="r_scales%d" % s, align_bytes=64)
            nc.vector.quantize_mx(
                out=r_codes[s][:, cols].bitcast(E4M3X4),
                scales=r_scales[s][:, cols],
                in_=r_grouped[s][:, PACK * cols.start : PACK * cols.stop],
            )

        def spread_q(h):
            bank = psum.tile([P, PACK, P], F32, name="q_bank%d" % h, tag="bank%d" % unit_bank(PACK - 1 - h))
            for c in range(PACK):
                nc.tensor.transpose(bank[:, c, :], q_cols32[:, h, c : c + 1].to_broadcast([P, P]), ident[:])
            nc.scalar.copy(q_rows[h][:].rearrange("p (n c) -> p n c", c=PACK), bank[:].rearrange("p c n -> p n c"))


        def multiply(n, passes=range(PASSES)):
            e, g, h, t = place(n)
            s = g * PACK + t
            if passes.start == 0:
                inter[n] = psum.tile([P, N], F32, name="inter%d" % n, tag="bank%d" % unit_bank(n))
            for k in passes:
                nc.tensor.matmul_mx(
                    out=inter[n][:],
                    lhsT=r_codes[s][:, k * P : (k + 1) * P].bitcast(E4M3X4),
                    lhsT_scale=r_scales[s][:, k * P : (k + 1) * P],
                    rhs=g_words[h, k].bitcast(E5M2X4),
                    rhs_scale=g_scales[h][:, k, :],
                    start=(k == 0),
                    stop=(k == PASSES - 1),
                )

        def subtract(n, cols=WHOLE):
            e, g, h, t = place(n)
            if cols.start == 0:
                q_less_inter[n] = work.tile([P, N], F32, name="q_less_inter%d" % n, tag="q_less_inter")
            nc.vector.tensor_tensor(
                out=q_less_inter[n][:, cols], in0=q_rows[h][:, cols], in1=inter[n][:, cols], op=ALU.subtract
            )

        def root(n, cols=WHOLE):
            e, g, h, t = place(n)
            s = g * PACK + t
            if cols.start == 0:
                inv_root[n] = work.tile([P, N], F32, name="inv_root%d" % n, tag="inv_root")
            nc.scalar.activation(
                inv_root[n][:, cols],
                q_less_inter[n][:, cols],
                ACT.Abs_reciprocal_sqrt,
                bias=r_over_gain[:, s : s + 1],
                scale=inv_gain[:, s : s + 1],
            )

        def square(n, cols=WHOLE):
            if cols.start == 0:
                gain_over_union[n] = work.tile([P, N], F32, name="gain_over_union%d" % n, tag="gain_over_union")
            nc.scalar.activation(gain_over_union[n][:, cols], inv_root[n][:, cols], ACT.Square)

        def finish(n, cols=WHOLE):
            e, g, h, t = place(n)
            if t == 0 and cols.start == 0:
                y_sets[e] = work.tile([P, PACK, N], F32, name="y_set%d" % e, tag="y_set")
            nc.vector.tensor_tensor(
                out=y_sets[e][:, t, cols], in0=inter[n][:, cols], in1=gain_over_union[n][:, cols], op=ALU.mult
            )


        def turn_y(e, b, bank, slots=range(PACK)):
            if slots.start == 0:
                y_banks[e, b] = psum.tile([P, PACK, P], F32, name="y_bank%d_%d" % (e, b), tag="bank%d" % bank)
            for t in slots:
                nc.tensor.transpose(y_banks[e, b][:, t, :], y_sets[e][:, t, b * P : (b + 1) * P], ident[:])

        def store_y(e, b, engine):
            g, h = divmod(e, HALVES)
            rows = work.tile([P, P, PACK], F32, name="y_rows%d_%d" % (e, b), tag="y_rows", bufs=8)
            copy_on(engine, rows[:], y_banks[e, b][:].rearrange("i t p -> i p t"))
            i0 = h * N + b * P
            nc.sync.dma_start(out=out_0[i0 : i0 + P, g * N : (g + 1) * N], in_=rows[:].rearrange("i p t -> i (p t)"))

        def round_on_gpsimd(e, a):
            y_grouped[e, a] = work.tile(
                [P, N // 2, PACK], BF16, name="y_grouped%d_%d" % (e, a), tag="y_gpsimd", bufs=1, align_bytes=64
            )
            part = y_sets[e][:, :, (LEFT, RIGHT)[a]]
            nc.gpsimd.tensor_scalar(y_grouped[e, a][:], part.rearrange("p t i -> p i t"), 1.0, 0.0, ALU.mult, ALU.add)

        def round_on_vector(e, a):
            y_grouped[e, a] = work.tile(
                [P, N // 2, PACK], BF16, name="y_grouped%d_%d" % (e, a), tag="y_vector", bufs=2, align_bytes=64
            )
            part = y_sets[e][:, :, (LEFT, RIGHT)[a]]
            nc.vector.tensor_copy(
                y_grouped[e, a][:].rearrange("p (c i) t -> p c t i", i=4),
                part.rearrange("p t (c i) -> p c t i", i=4),
            )

        def quantize_y(e, a):
            g, h = divmod(e, HALVES)
            if a == 0:
                y_codes[e] = work.tile([P, N], U32, name="y_codes%d" % e, tag="y_codes", align_bytes=64)
            if a == 0 and h == 0:
                y_scales[g] = keep.tile([P, QUERIES], U8, name="y_scales%d" % g, align_bytes=64)
            cols = (LEFT, RIGHT)[a]
            nc.vector.quantize_mx(
                out=y_codes[e][:, cols].bitcast(E4M3X4),
                scales=y_scales[g][:, h * N + cols.start : h * N + cols.stop],
                in_=y_grouped[e, a][:].rearrange("p i t -> p (i t)"),
            )
            if a == 1:
                codes_hbm = out_1[g].rearrange("p n t -> p (n t)").bitcast(I32)
                nc.sync.dma_start(out=codes_hbm[:, h * N : (h + 1) * N], in_=y_codes[e][:].bitcast(I32))
            if a == 1 and h == HALVES - 1:
                for quad in range(QUADS):
                    nc.sync.dma_start(
                        out=out_2[g, 4 * quad : 4 * quad + 4, :].bitcast(I32),
                        in_=y_scales[g][32 * quad : 32 * quad + 4, :].bitcast(I32),
                    )

        nc.scalar.activation(gain_root[:], gain_cols[:], ACT.Abs_reciprocal_sqrt)
        nc.scalar.activation(gain_guess[:], gain_root[:], ACT.Square)
        sort_half(0, 0)
        sort_half(0, 1)
        turn_slot(0)
        empty_half(0, 0, "scalar")
        empty_half(0, 1, "scalar")
        nc.vector.tensor_copy(q_cols32[:], q_cols[:])
        sort_half(1, 0)
        sort_half(1, 1)
        turn_slot(1)
        quantize_slot(0, LEFT)
        nc.vector.scalar_tensor_tensor(
            out=gain_check[:], in0=gain_guess[:], scalar=-1.0, in1=gain_cols[:], op0=ALU.mult, op1=ALU.mult
        )
        quantize_slot(0, RIGHT)
        nc.vector.scalar_tensor_tensor(
            out=inv_gain[:], in0=gain_check[:], scalar=2.0, in1=gain_guess[:], op0=ALU.add, op1=ALU.mult
        )
        empty_half(1, 0, "scalar")
        empty_half(1, 1, "vector")
        spread_q(0)
        quantize_slot(1)

        multiply(0, range(0, 2))
        spread_q(1)
        sort_half(2, 1)
        turn_slot(2)
        multiply(0, range(2, PASSES))
        multiply(1)
        empty_half(2, 0, "scalar")
        empty_half(2, 1, "vector")
        nc.vector.tensor_tensor(out=r_over_gain[:], in0=r_cols[:], in1=inv_gain[:], op=ALU.mult)
        subtract(0)
        quantize_slot(2)
        sort_half(3, 1)
        turn_slot(3)
        root(0)
        subtract(1)
        sort_half(4, 1)

        for n in (2, 3):
            multiply(n)
            empty_half(n + 1, 0, "scalar")
            empty_half(n + 1, 1, "scalar")
            square(n - 2)
            root(n - 1)
            turn_slot(n + 2)
            quantize_slot(n + 1)
            subtract(n)
            finish(n - 2)
            sort_half(n + 3, 1)
        square(2)

        for c in range(2, LATE_UNIT // 2):
            first, second = 2 * c, 2 * c + 1
            e, a = divmod(c - 2, 2)
            old_e, old_a = divmod(c - 3, 2)
            has_old = c > 2
            s = c + SLOT_LEAD
            multiply(first)
            multiply(second)
            if has_old:
                store_y(old_e, 2 * old_a, "vector")
            empty_half(s - 1, 0, "scalar")
            root(first - 1)
            finish(first - 2)
            empty_half(s - 1, 1, "scalar")
            subtract(first)
            square(first - 1)
            quantize_slot(s - 1)
            finish(first - 1)
            root(first)
            if s + 1 < SLOTS and c % 2 == 0:
                sort_half(s + 1, 1)
            if has_old:
                quantize_y(old_e, old_a)
            round_on_gpsimd(e, a)
            subtract(second)
            if has_old:
                store_y(old_e, 2 * old_a + 1, "scalar")
            square(first)
            if s < SLOTS:
                turn_slot(s)
            else:
                multiply(LATE_UNIT)
            turn_y(e, 2 * a, Y_BANK)
            turn_y(e, 2 * a + 1, Y_BANK + 1)

        last_set, last = SETS - 1, UNITS - 1
        multiply(LATE_UNIT + 1)
        for n in range(LATE_UNIT, last):
            e, a = divmod(n // 2 - 3, 2)
            root(n - 1)
            subtract(n)
            finish(n - 2)
            if n + 2 < last:
                multiply(n + 2)
            if n % 2 == 0:
                store_y(e, 2 * a + 1, "scalar")
                store_y(e, 2 * a, "vector")
            else:
                quantize_y(e, a)
                next_e, next_a = divmod(n // 2 - 2, 2)
                round_on_gpsimd(next_e, next_a)
            square(n - 1)
            if n == LATE_UNIT:
                turn_y(e, 2, Y_BANK)
                turn_y(e, 3, Y_BANK + 1)
            if n + 2 == last:
                banks = (Y_BANK, Y_BANK + 1, unit_bank(n - 3), unit_bank(n - 2))
                for b in range(PACK):
                    if b == 2:
                        multiply(last)
                    turn_y(last_set - 1, b, banks[b])

        root(last - 1)
        subtract(last, LEFT)
        subtract(last, RIGHT)
        quantize_y(last_set - 1, 0)
        round_on_gpsimd(last_set - 1, 1)
        finish(last - 2)
        root(last, LEFT)
        square(last - 1)
        root(last, RIGHT)
        store_y(last_set - 1, 2, "vector")
        finish(last - 1)
        square(last, LEFT)
        square(last, RIGHT)
        store_y(last_set - 1, 3, "scalar")
        banks = (unit_bank(last - 3), unit_bank(last - 2), Y_BANK, Y_BANK + 1)
        for slots in (range(0, 2), range(2, 3)):
            for b in range(PACK):
                turn_y(last_set, b, banks[b], slots)
        finish(last, LEFT)
        finish(last, RIGHT)
        for b in range(PACK):
            turn_y(last_set, b, banks[b], range(3, PACK))
        quantize_y(last_set - 1, 1)
        store_y(last_set, 0, "scalar")
        round_on_vector(last_set, 0)
        store_y(last_set, 1, "scalar")
        round_on_vector(last_set, 1)
        store_y(last_set, 2, "scalar")
        quantize_y(last_set, 0)
        quantize_y(last_set, 1)
        store_y(last_set, 3, "scalar")
